import numpy as np, ml_dtypes
CORES = [2,3,42,43,82,83,122,123]
N = 8
import mx_ref
BF = ml_dtypes.bfloat16
def gentries(a):
    return np.ascontiguousarray(a.reshape(8, 16, -1).transpose(0, 2, 1)).reshape(8, -1)
def gtable(e):
    e = np.asarray(e); return np.ascontiguousarray(e.reshape(8, -1, 16).transpose(0, 2, 1)).reshape(128, -1).astype(np.int32)
def gcols(t, e):
    v = np.concatenate([t.reshape(8, 16, -1, 4), np.zeros((8, 16, 1, 4), BF)], axis=2)
    return np.ascontiguousarray(np.stack([v[g][:, e[g]] for g in range(8)])).reshape(128, -1)
def tile(rs):
    return np.stack(rs, axis=2).reshape(128, -1).astype(BF)
def cut(t, i, w=512):
    return t[:, w * i:w * i + w]
def pick(q, e):
    c = np.concatenate([q[0].reshape(128, -1, 4), np.zeros((128, 1, 4), np.uint8)], axis=1); s = np.concatenate([q[1], np.ones((16, 1), np.uint8)], axis=1)
    return (np.ascontiguousarray(c[:, e].reshape(128, -1)), np.ascontiguousarray(s[:, e]))
def join(*qs):
    return (np.concatenate([q[0] for q in qs], axis=1), np.concatenate([q[1] for q in qs], axis=1))
def put(q, e, v):
    c, s = q[0].reshape(128, -1, 4).copy(), q[1].copy(); c[:, e] = v[0].reshape(128, -1, 4); s[:, e] = v[1]
    return (c.reshape(128, -1), s)
def pk(c, s):
    return (np.ascontiguousarray(c), mx_ref.live(s))
def emit(q):
    return q[0], q[1]
def packed(v, rng):
    q = [mx_ref.quantize(np.ascontiguousarray(v[r])) for r in range(N)]
    return np.stack([a for a, b in q]), np.stack([mx_ref.plane(b, rng) for a, b in q])
def values_of_codes():
    e, c = np.zeros((128, 128, 4), np.float32), np.zeros((128, 2, 4), np.uint8)
    e[np.arange(128), np.arange(128), 0] = 1
    c[:127, :, 0] = np.arange(256).reshape(2, 128).T[:127]
    return mx_ref.matmul(mx_ref.quantize(e.reshape(128, 512).astype(BF)), (c.reshape(128, 8), np.full((16, 2), 127, np.uint8))).T.reshape(-1).astype(np.float64)
CODE_VALUE, SCALE_VALUE = values_of_codes(), 2.0 ** (np.arange(256) - 127.0)
def decode(q):
    return (CODE_VALUE[q[0]].reshape(16, 8, -1, 4) * SCALE_VALUE[q[1]][:, None, :, None] + 0.0).reshape(128, -1).astype(np.float32)
def f(rng, *shape):
    return mx_ref.flush((rng.standard_normal(shape, dtype=np.float32) * np.exp2(rng.integers(-2, 3, shape[:-1] + (1,)))).astype(BF))
def wide(rng, *shape, cols=0):
    v = rng.standard_normal(shape, dtype=np.float32) * np.exp2(rng.integers(-12, 13, shape)).astype(np.float32)
    if cols: v *= np.repeat(np.exp2(rng.integers(-cols, cols + 1, shape[:-2] + (1, shape[-1] // 4))) * (rng.random(shape[:-2] + (1, shape[-1] // 4)) > 0.0625), 4, axis=-1).astype(np.float32)
    return mx_ref.flush(v.astype(BF))
C, K, R = 256, 64, 3
def order(p):
    return np.argsort(-(p[::16] + np.float32(0.0)), axis=1, kind="stable")
def larger(a, b):
    return np.maximum(a.astype(np.float32), b.astype(np.float32)).astype(BF)
def numbers_of(rng):
    return {"x": np.array(f(rng, N, 128, 4 * C)), "u": np.array(f(rng, N, 128, 512)), "v": np.array(f(rng, N, 128, 512))}
def weights(rng, still=[]):
    w = np.array(f(rng, N, 128, 2048)).reshape(N, 8, 16, 4, 8, 16, 4)
    for i in still:
        w[:, :, i] = 0
        w[:, :, :, :, :, i] = 0
    c, p = packed(w.reshape(N, 128, 2048), rng)
    return {"wc": c, "ws": p}
def lists_of(rng):
    return np.stack([gtable(rng.integers(0, C, (8, R * C))) for r in range(N)])
def signs(rng):
    return np.stack([rng.permutation(8) % 2 * 2.0 - 1.0 for r in range(N)])
def setup_inputs(rng):
    return {**numbers_of(rng), **weights(rng), "nb": lists_of(rng)}
def setup_inputs_ties(rng):
    d = numbers_of(rng)
    e = rng.permutation(N)
    x = d["x"].reshape(N, 8, 16, C, 4)
    for r in range(N):
        k = np.zeros(C, int) if r == e[0] else rng.permutation(C) % 3
        a = x[r][:, :8, :3].copy()
        a[:, :, 2] = 0
        x[r][:, :8] = a[:, :, k]
    x[e[1]][:, :8] = 0
    u = d["u"].reshape(N, 8, 16, 8, 16, 4)
    k = u.copy()
    u[:, :, :, :, :3] = 0
    for g in range(8): u[:, g, :8, g, :3] = k[:, g, :8, g, :3]
    return {"x": x.reshape(N, 128, 4 * C), "u": u.reshape(N, 128, 512), "v": d["v"], **weights(rng, range(8)), "nb": lists_of(rng)}
def setup_inputs_near(rng):
    d = numbers_of(rng)
    x = d["x"].astype(np.float32).reshape(N, 8, 16, C, 4)
    u = d["u"].reshape(N, 128, 128, 4)
    x[:, :, 0] = 0
    x[:, :, 10] = 0
    for i in range(3): u[:, :, i::16] = 0
    c = rng.permutation(8) % 2 * 2.0 - 1.0
    first = int(rng.integers(N))
    upper = np.arange(C) // (C // 2)
    for n in range(N):
        r = (first + n) % N
        i = (np.arange(C) + rng.integers(0, C, (8, 1))) % (C // 2) * 2 + upper
        one = n < N // 2
        s = i // 2 if one else i
        size = 1.0 if one else 2.0 ** -7
        k = 1.0 if one and n % 2 == 0 else 2.0 ** -30
        if one:
            x[r, :, 0, :, 0] = c[:, None]
            for g in rng.permutation(8)[:4]: x[r, g, 0, rng.integers(C), 0] *= np.float32(2.0 ** 30)
        z = ((s[:, :, None] >> np.arange(8)) & 1) * np.exp2(np.arange(8) - 23.0) * size
        x[r, :, 8] = z[:, :, :4]
        x[r, :, 9] = z[:, :, 4:]
        x[r, :, 10, :, 0] = rng.integers(-1, 2, (8, C)) * 2.0 ** -23 * size
        x[r, :, 11:] = rng.integers(4, 8, (8, 5, C, 4)) * rng.choice([-1.0, 1.0], (8, 5, C, 4)) * 2.0 ** -20 * size
        for h in range(0, 128, 16):
            u[r, h, h:h + 2, 0] = k
            u[r, h + 8:h + 10, h] = k
            u[r, h + 8:h + 10, h + 1] = (k * rng.choice([-1.0, 1.0], (2, 4))).astype(np.float32).astype(BF)
            u[r, h + 10, h + 2, 0] = k
    return {"x": x.reshape(N, 128, 4 * C).astype(BF), "u": u.reshape(N, 128, 512), "v": d["v"], **weights(rng, [0, 8, 9, 10, 11, 12, 13, 14, 15]), "nb": lists_of(rng)}
def setup_inputs_huge(rng):
    d = numbers_of(rng)
    c = np.stack([rng.permutation(C) % 2 * 2.0 - 1.0 for r in range(N)])
    low = (int(rng.integers(N)) + np.arange(N // 2)) % N
    c[low] = -1
    size = np.where(c < 0, -2.0 ** 30, 2.0 ** 28)
    size[low, C - K:] *= 0.7
    x = (0.6 + 0.2 * rng.random((N, 128, C, 4))) * size[:, None, :, None]
    u = d["u"].reshape(N, 128, 128, 4)
    for i in range(3):
        a = 2.0 ** 30 * (1 - 0.25 * rng.random((N, 128, 8, 4))) * signs(rng)[:, None, :, None]
        u[:, :, i::16] = a.astype(np.float32).astype(BF)
    w = np.zeros((N, 128, 4, 128, 4), np.float32)
    i = np.arange(128)
    for b in range(4): w[:, i, b, i, b] = 16 - 32 * (i % 2)
    wc, ws = packed(w.reshape(N, 128, 2048).astype(BF), rng)
    return {"x": x.astype(np.float32).reshape(N, 128, 4 * C).astype(BF), "u": u.reshape(N, 128, 512), "v": d["v"], "wc": wc, "ws": ws, "nb": lists_of(rng)}
def setup_inputs_chains(rng):
    d = numbers_of(rng)
    x = d["x"].astype(np.float32).reshape(N, 8, 16, C, 4)
    u = d["u"].reshape(N, 128, 128, 4)
    h, e, k = rng.permutation(8).tolist(), rng.permutation(N), np.arange(N)[:, None]
    x[:, :, :3] = 0
    x[:, :, 0, :, 0] = rng.integers(1, 8, (N, 8, C))
    x[:, h[0], 0, :, 0] = 1 + k
    x[:, h[1], 0, :, 0] = N - k
    x[:, :, 1, :, 0] = rng.integers(1, 16, (N, 8, C))
    x[:, :, 2, :, 0] = rng.integers(-1, 2, (N, 8, C))
    x[e[0], :, 2, :, 0] = 0
    x[e[1], :, 2, :, 0] = -1
    for i in range(3): u[:, :, i::16] = 0
    for g in range(8):
        i = 16 * g
        u[:, i + (0 if g in h[2:6] else 1), i, 0] = -1 if g in h[4:6] else 1
        u[:, i, i + 1, 0] = 1
        u[:, i + 2, i + 2, 0] = 1
    nb = rng.integers(0, C, (N, 8, R, C))
    for r in range(N):
        q = rng.permutation(8)
        nb[r, q[0]] = rng.integers(0, C)
        nb[r, q[1]] = np.arange(C)
        nb[r, q[2]] = C - 1 - np.arange(C)
        nb[r, q[3]] = (np.arange(C) + 1) % C
    nb = np.stack([gtable(nb[r].reshape(8, R * C)) for r in range(N)])
    return {"x": x.reshape(N, 128, 4 * C).astype(BF), "u": u.reshape(N, 128, 512), "v": d["v"], **weights(rng, [0, 1, 2]), "nb": nb}
def setup_inputs_spread(rng):
    d = setup_inputs(rng)
    d["x"] = wide(rng, N, 128, 4 * C, cols=6)
    return d
def check_inputs(d):
    b = []
    for k in ("x", "u", "v"):
        a = np.abs(d[k].astype(np.float32))
        if not (np.isfinite(a).all() and ((a == 0) | (a >= 2.0 ** -30) & (a <= 2.0 ** 30)).all()): b.append("a value of " + k)
    if ((d["wc"] & 0x7F) == 0x7F).any(): b.append("a code of wc that is no number")
    none, least, most = [emit(mx_ref.quantize(np.full((128, 16), k, np.float32).astype(BF)))[1][0, 0] for k in (0.0, 2.0 ** -30, 2.0 ** 30)]
    for r in range(N):
        s = mx_ref.live(d["ws"][r])
        if ((s != none) & ((s < least) | (s > most))).any(): b.append("a scale of ws")
    if (d["nb"] < 0).any() or (d["nb"] >= C).any(): b.append("an entry of nb")
    return b
def reference(x, u, v, wc, ws, nb):
    qu = [mx_ref.quantize(u[r]) for r in range(N)]
    lay = [pk(wc[r], ws[r]) for r in range(N)]
    now = [x[r] for r in range(N)]
    far = [gentries(nb[r]).reshape(8, R, C) for r in range(N)]
    guests = [np.zeros((128, 0), BF) for r in range(N)]
    place = np.arange(C)
    p = np.zeros((N, 8, C), np.int64) + place
    for t in range(R):
        sent = []
        for r in range(N):
            s = mx_ref.matmul(qu[r], mx_ref.quantize(now[r]))
            p[r] = np.where(s[2::16] < 0, place, p[r])
            sent.append(mx_ref.quantize(gcols(now[r], order(s)[:, :K])))
        came = decode(join(*sent)).astype(BF)
        for r in range(N):
            guests[r] = np.concatenate([guests[r], cut(came, (r - 1) % N, 4 * K)], axis=1)
            pool = np.concatenate([now[r], guests[r]], axis=1)
            cand = np.stack([p[r], np.take_along_axis(p[r], far[r][:, t], axis=1), np.zeros((8, C), np.int64) + C + K * t + place % K])
            met = [larger(now[r], gcols(pool, cand[k])) for k in range(3)]
            best = np.argmax(np.stack([mx_ref.matmul(qu[r], mx_ref.quantize(met[k]))[1::16] + np.float32(0.0) for k in range(3)]), axis=0)
            p[r] = np.take_along_axis(cand, best[None], axis=0)[0]
            q = mx_ref.quantize(gcols(np.concatenate(met, axis=1), best * C + place))
            now[r] = tile([np.maximum(mx_ref.matmul(pick(lay[r], np.arange(128 * b, 128 * b + 128)), q), np.float32(0.0)) * np.float32(0.015625) + now[r][:, b::4].astype(np.float32) for b in range(4)])
    y, op = np.zeros((N, 128, C), np.float32), np.zeros((N, 8, C), np.float32)
    oc, osc = np.zeros((N, 128, 4 * C), np.uint8), np.zeros((N, 16, C), np.uint8)
    for r in range(N):
        q = mx_ref.quantize(now[r])
        y[r] = mx_ref.matmul(mx_ref.quantize(v[r]), q)
        op[r] = p[r]
        oc[r], osc[r] = emit(q)
    return {"y": y, "op": op, "oc": oc, "osc": osc}

import numpy as np
from concourse.bass import DstId, RemoteDMATransfer
from concourse.mybir import dt, AluOpType, ActivationFunctionType

C, K, R = 256, 64, 3
BF, F32, I32, U16, Q4, U8 = "bfloat16", "float32", "int32", "uint16", "float8_e4m3fn_x4", "uint8"
SCRATCH = {}
for _d, _names in (
        (BF, "pool 1536 jj 3072 zt 1024 gt 512 g0 1024 xc 1024 ut 512 vt 512 ct 5120 zero 512 ones 516 eb 516 ai 512 at 1024 rs16 256 rs64 256 rs128 256 "
             "four 512 ne 1024 st 1024 fm 256 fs 256 c1 256 c1s 256 c2 256 c2s 256"),
        (F32, "pq 8 col 32 k4 8 jf 256 mmin 256 mbig 256 mzer 256 rmin 256 sm 256 sa 256 sn 16 pm 256 ps 256 s0m 256 m01 256 bc 64 zz 64 "
              "cw 2304 fw 4096 p4 1024 po 256 rr 1024 yo 256"),
        (I32, "nbi 48 uli 24 di 256 ri 256 pi 8 d4 256 r4 256"),
        (U16, "nbo 48 ulo 24 og 16 of 16 oj 64 oz 64 ow 64"),
        (Q4, "uq 128 u3q 384 vq 128 wq 512 xq 256 jq 768 zq 256 gq 256 cq 1280 eq 512 aq 256 lq0 192 lq1 192 lq2 192"),
        (U8, "us 128 u3s 384 vs 128 wsc 512 xs 256 js 768 zs 256 gs 256 cs 1280 es 512 asc 256 ls0 384 ls1 384 ls2 384")):
    _l = _names.split()
    for _i in range(0, len(_l), 2):
        SCRATCH[_l[_i]] = ("sbuf", [128, int(_l[_i + 1])], _d)
for _b in range(8):
    SCRATCH["b%d" % _b] = ("psum", [128, 512], F32)
SEMAPHORES = ["V", "S", "P", "G"] + ["d%d" % i for i in range(24)] + ["arr%d" % t for t in range(R)] + ["snt%d" % t for t in range(R)]

AL, AF = AluOpType, ActivationFunctionType
PLAN = {"tiles": [[(0, "v"), (1, "v"), (2, "s"), (3, "s")], [(1, "s"), (0, "v"), (2, "s"), (3, "s")], [(1, "s"), (0, "v"), (2, "s"), (3, "s")]],
        "fix": 50.0, "cyc": 1.0, "gat": 1.56, "wake": 60.0, "pe": 0.6, "dma": 2000.0, "rem": 3000.0, "first": 1500.0, "turns": 6, "zv": 512}


def rank_program(g, core, T, topo):
    rank = T.rank_of(core)
    if rank is None:
        return
    n = len(T.cores)
    nxt, prv = T.cores[(rank + 1) % n], T.cores[(rank - 1) % n]
    ops, last_w, readers, ndma, sent = [], {}, {}, [0], {}
    queue = {"V": g.vector, "S": g.scalar, "P": g.tensor, "G": g, "Y": g.sync}

    def w(name, a=0, b=None, s=1):
        return (name, a, SCRATCH[name][1][1] if b is None else b, s)

    def ap(v):
        return T[v[0]][:, v[1]:v[2]:v[3]] if v[3] != 1 else T[v[0]][:, v[1]:v[2]]

    def add(eng, fn, rd, wr, cost, lat=0.0, kind="c", sem=None, cnt=1, chain=False, after=()):
        me, deps, soft = len(ops), set(), set(after)
        for v, writes in [(v, False) for v in rd] + [(v, True) for v in wr]:
            bank = SCRATCH[v[0]][0] == "psum"
            width = 1 if bank else SCRATCH[v[0]][1][1]
            lw = last_w.setdefault(v[0], np.full(width, -1))
            rs = readers.setdefault(v[0], [])
            cols = np.zeros(width, bool)
            cols[slice(0, 1) if bank else slice(v[1], v[2], v[3])] = True
            for o in set(lw[cols].tolist()):
                if o >= 0:
                    (soft if chain and bank else deps).add(o)
            for o, c in rs:
                if (writes or (bank and ops[o]["eng"] != eng)) and o != me and (c & cols).any():
                    deps.add(o)
            if writes:
                lw[cols] = me
                readers[v[0]] = [(o, c & ~cols) for o, c in rs if (c & ~cols).any()]
            else:
                rs.append((me, cols))
        deps.discard(me)
        ops.append({"eng": eng, "fn": fn, "deps": deps, "soft": soft, "kind": kind, "sem": sem, "cnt": cnt, "inc": False, "cost": cost, "lat": lat})
        return me

    def val(x):
        return ap(x) if isinstance(x, tuple) else x

    def tup(*xs):
        return [x for x in xs if isinstance(x, tuple)]

    def src(v, off):
        return ap(v).indirect(ap(off)) if off else ap(v)

    def size(v):
        return len(range(v[1], v[2], v[3]))

    def price(out, ins, per=None, off=None):
        if off:
            per = PLAN["gat"]
        elif per is None:
            per = 0.5 if all(SCRATCH[v[0]][2] in (BF, U16) for v in [out] + ins) else 1.0
        return PLAN["fix"] + size(out) * per * PLAN["cyc"]

    def dma(eng, out, in_, rd, wr, more=0.0):
        s = "d%d" % ndma[0]
        ndma[0] += 1
        add(eng, lambda: queue[eng].dma_start(out, in_), rd, wr, 60.0, PLAN["dma"] + more, kind="d", sem=s, cnt=16)

    def memset(v, c):
        add("V", lambda: g.vector.memset(ap(v), c), [], [v], price(v, []))

    def ts(out, in0, s1, op0, s2=None, op1=None):
        if op1 is None:
            add("V", lambda: g.vector.tensor_scalar(ap(out), ap(in0), val(s1), None, op0), tup(in0, s1), [out], price(out, [in0]))
        else:
            add("V", lambda: g.vector.tensor_scalar(ap(out), ap(in0), val(s1), val(s2), op0, op1), tup(in0, s1, s2), [out], price(out, [in0]))

    def tt(out, in0, in1, op, off=None):
        per = 1.0 if SCRATCH[in0[0]][0] == "psum" else 2.0
        add("V", lambda: g.vector.tensor_tensor(ap(out), src(in0, off), ap(in1), op), tup(in0, in1, off), [out], price(out, [], per, off))

    def scan(out, d0, d1, init, op0, op1):
        add("V", lambda: g.vector.tensor_tensor_scan(ap(out), ap(d0), ap(d1), init, op0, op1), [d0, d1], [out], price(out, [d0, d1]))

    def copy(eng, out, in_, off=None):
        if eng == "V":
            add("V", lambda: g.vector.tensor_copy(ap(out), src(in_, off)), tup(in_, off), [out], price(out, [in_], None, off))
        else:
            add("S", lambda: g.scalar.activation(ap(out), src(in_, off), AF.Copy), tup(in_, off), [out], price(out, [], 1.0, off) + 15)

    def act(out, in_, func, bias=0.0, scale=1.0):
        add("S", lambda: g.scalar.activation(ap(out), ap(in_), func, bias=val(bias), scale=scale), tup(in_, bias), [out], price(out, [], 1.0) + 15)

    def quant(q, s, a, b, tile):
        add("V", lambda: g.vector.quantize_mx(ap(w(q, a, b)), ap(w(s, a, b)), ap(tile)), [tile], [w(q, a, b), w(s, a, b)], 12 + 0.265 * size(tile) * PLAN["cyc"])

    def mm(bank, lq, ls, la, rq, rs, ra, rb, start=True, stop=True):
        o, l1, l2, r1, r2 = w(bank, 0, rb - ra), w(lq, la, la + 128), w(ls, la, la + 128), w(rq, ra, rb), w(rs, ra, rb)
        add("P", lambda: g.tensor.matmul_mx(ap(o), ap(l1), ap(l2), ap(r1), ap(r2), start, stop), [l1, l2, r1, r2], [o], (rb - ra + 16) * PLAN["pe"], 60.0, chain=not start)

    def iota(v, pattern, base, cm, after=()):
        cost = 130 + 2 * size(v) * PLAN["cyc"]
        if SCRATCH[v[0]][2] == I32:
            add("G", lambda: g.iota(ap(v), pattern, base, cm), [], [v], cost, after=after)
        else:
            add("G", lambda: g.iota(ap(v), pattern, base, cm, allow_small_or_imprecise_dtypes=True), [], [v], cost, after=after)

    def pick_u(a, b):
        off = T.ulo[:, a // 16:b // 16]
        add("V", lambda: g.vector.tensor_copy(T.u3q[:, a:b].bitcast(dt.uint32), T.uq[:, 0:128].bitcast(dt.uint32).indirect(off)),
            [w("uq"), w("ulo")], [w("u3q", a, b)], price(w("u3q", a, b), [], None, True))
        add("S", lambda: g.scalar.activation(T.u3s[:, a:b], T.us[:, 0:128].indirect(off), AF.Copy), [w("us"), w("ulo")], [w("u3s", a, b)], price(w("u3q", a, b), [], None, True))

    X = w("pool", 0, 1024)

    dma("S", T.ut[:], T.u[:], [], [w("ut")], 600.0)
    dma("Y", ap(X), T.x[:], [], [X], 1300.0)
    dma("Y", T.nbi[:], T.nb[:], [X], [w("nbi")])
    dma("Y", ap(w("jj", 2048, 3072)), T.x[:], [X], [w("jj", 2048, 3072)])
    dma("Y", T.wq[:].bitcast(dt.uint8), T.wc[:], [X], [w("wq")])
    dma("Y", T.wsc[:], T.ws[:], [X], [w("wsc")])
    dma("Y", T.vt[:], T.v[:], [X], [w("vt")])

    iota(w("uli"), [[1, 3], [16, 8]], 0, 0)
    iota(w("di"), [[-1, 256]], 256, 1)
    iota(w("pi"), [[0, 8]], 0, 1)
    iota(w("ai"), [[16, 8], [0, 64]], 0, 0)
    iota(w("k4"), [[1, 8]], 0, 0)
    iota(w("jf"), [[1, 256]], 0, 0)
    iota(w("d4"), [[-4, 256]], 1024, 1)
    iota(w("cw", 512, 768), [[1, 256]], 0, 0)
    memset(w("ones"), 1.0)
    add("G", lambda: g.affine_select(T.eb[:], T.ones[:], [[1, 516]], AL.is_equal, 0.0, -3, -4), [w("ones")], [w("eb")], 1200.0)
    iota(w("cw", 0, 256), [[0, 4], [1, K]], C, 0)

    memset(w("zero"), 0.0)
    memset(w("ct", 4096, 5120), 0.0)
    memset(w("rmin"), 5e29)
    copy("V", w("ulo"), w("uli"))
    memset(w("rmin", 0, 256, 16), -5e29)
    for t in range(R):
        quant("lq%d" % t, "ls%d" % t, 0, 128, w("zero"))
    quant("gq", "gs", 128, 256, w("zero"))
    memset(w("gt", 256, 512), 0.0)
    ts(w("ri"), w("di"), 15, AL.bitwise_and)
    ts(w("r4"), w("d4"), 2, AL.arith_shift_right, 3, AL.bitwise_and)
    quant("uq", "us", 0, 128, w("ut"))
    ts(w("mmin"), w("ri"), -2e28, AL.mult, 1e28, AL.add)
    pick_u(0, 128)
    pick_u(128, 384)
    q = w("col", 15, 16)
    copy("V", q, w("ri", 0, 1))
    memset(w("four"), 4.0)
    ts(w("pq"), w("pi"), q, AL.subtract)
    ts(w("col", 14, 15), q, -1024.0, AL.mult)
    ts(w("at", 0, 512), w("ai"), w("pq", 0, 1), AL.is_equal)
    ts(w("col", 0, 4), w("k4", 0, 4), -16384.0, AL.mult, w("col", 14, 15), AL.add)
    quant("aq", "asc", 0, 128, w("at", 0, 512))
    comps = sorted(set(sum(m == "c" for i, m in tl) for tl in PLAN["tiles"]) - {0})
    for m in comps:
        ts(w("col", 16 + 4 * m, 20 + 4 * m), w("col", 0, 4), 65536.0 * m, AL.add)
    if comps:
        ts(w("at", 512, 1024), w("ai"), w("pq", 0, 1), AL.is_equal, -1.0, AL.mult)
        quant("aq", "asc", 128, 256, w("at", 512, 1024))
    ts(w("col", 4, 5), q, 2048.0, AL.add)
    ts(w("col", 8, 9), q, 4.0, AL.mult, 1024.0, AL.add)
    ts(w("col", 9, 10), w("r4", 0, 1), 512.0, AL.add)
    ts(w("mbig"), w("r4"), 2e28, AL.mult, -1e28, AL.add)
    for name, step, den in (("rs16", 16, 256), ("rs64", 4, 256), ("rs128", 4, 512)):
        memset(w(name), -1e29)
        ts(w(name, 0, 256, step), w("jf", 0, 256, step), 1.0 / den, AL.mult)
    copy("V", w("nbo"), w("nbi"))
    for b in range(4):
        quant("eq", "es", 128 * b, 128 * b + 128, w("eb", 3 - b, 515 - b))
    ts(w("mzer"), w("ri"), -1e28, AL.mult)
    quant("vq", "vs", 0, 128, w("vt"))

    engs, back = topo.engines(core, nxt), topo.engines(prv, core)
    half = len(engs) // 2
    masks = [sum(1 << e for e in engs[:half]), sum(1 << e for e in engs[half:2 * half])]
    rid, pid = topo.addr(nxt)[0], topo.addr(nxt)[1]

    def send(t):
        def fn():
            return g.remote_dma_fused([
                RemoteDMATransfer(dst_ids=[DstId(rid=rid, pnc=pid)], dma_engine_mask=masks[0], remote_sem=T.sem["arr%d" % t],
                                  src=T.gq[:, 0:64].bitcast(dt.uint8), dst=T["lq%d" % t][:, 128:192].bitcast(dt.uint8)),
                RemoteDMATransfer(dst_ids=[DstId(rid=rid, pnc=pid)], dma_engine_mask=masks[1], remote_sem=T.sem["arr%d" % t],
                                  src=T.gs[:, 0:256], dst=T["ls%d" % t][:, 128:384])], local_sem=T.sem["snt%d" % t])
        sent[t] = add("G", fn, [w("gq", 0, 64), w("gs")], [], 300.0, PLAN["rem"] + (0.0 if t else PLAN["first"]), kind="r", sem="snt%d" % t, cnt=2 * half)

    def arrive(t):
        add("A", None, [], [w("lq%d" % t, 128, 192), w("ls%d" % t, 128, 384)], 0.0, kind="a", sem="arr%d" % t, cnt=len(back) // 2 * 2, after=[sent[t]])

    def cmp_view(k, a, b):
        base = 1024 * (k // 4) + k % 4
        return w("ct", base + 4 * a, base + 4 * (b - 1) + 1, 4)

    def quant_ct(i):
        quant("cq", "cs", 256 * i, 256 * i + 256, w("ct", 1024 * i, 1024 * i + 1024))

    quant("xq", "xs", 0, 256, X)
    for t in range(R):
        cw = 768 * t
        mm("b0", "u3q", "u3s", 0, "xq", "xs", 0, 256)
        mm("b3", "u3q", "u3s", 0, "xq", "xs", 0, 256)
        mm("b1", "u3q", "u3s", 256 if t else 128, "xq", "xs", 0, 256)
        tt(w("sm"), w("b0", 0, 256), w("mmin"), AL.min)
        scan(w("sa"), w("rmin"), w("sm"), -5e29, AL.min, AL.max)

        tiles = PLAN["tiles"][t]
        ncomp = sum(m == "c" for i, m in tiles)
        if ncomp:
            act(w("sn"), w("sa", 15, 256, 16), AF.Copy, 0.0, -1.0)
        for i, m in tiles:
            for k in range(4 * i, 4 * i + 4):
                e, mine = min(16 * k + 17, C), w("sa", 16 * k + 15, 16 * k + 16)
                if m == "c":
                    ts(cmp_view(k, 0, e), w("b0", 0, e), mine, AL.is_ge)
                    act(cmp_view(k, e, C), w("b3", e, C), AF.Sign, w("sn", k, k + 1), 1.0)
                    continue
                if e < C:
                    ts(cmp_view(k, e, C), w("b0", e, C), mine, AL.is_le)
                if m == "v":
                    ts(cmp_view(k, 0, e), w("b0", 0, e), mine, AL.is_lt)
                else:
                    act(cmp_view(k, 0, e), w("b3", 0, e), AF.Sign, mine, -1.0)
            if m != "v":
                v = w("ct", 1024 * i + 4 * (64 * i + 17), 1024 * i + 1024) if m == "c" else w("ct", 1024 * i, 1024 * i + 4 * min(64 * i + 65, C))
                act(v, v, AF.Relu)
        tt(w("ct", 4100, 5120, 4), w("b0", 1, 256), w("sa", 0, 255), AL.is_equal)
        order = [(4, "v")] + tiles
        for m, (i, how) in enumerate(order):
            quant_ct(i)
            mm("b2", "aq", "asc", 128 if how == "c" else 0, "cq", "cs", 256 * i, 256 * i + 256, m == 0, m == len(order) - 1)
        kcol = 16 + 4 * ncomp if ncomp else 0
        for c in range(4):
            act(w("ne", 256 * c, 256 * c + 256), w("b2", 0, 256), AF.Abs, w("col", kcol + c, kcol + c + 1), 1024.0)
        scan(w("st", 0, 512), w("ne", 0, 512), w("four"), 0.0, AL.min, AL.add)
        scan(w("st", 512, 1024), w("ne", 512, 1024), w("four"), 0.0, AL.min, AL.add)
        for e in (2, 0, 3, 1):
            ts(w("og", 4 * e, 4 * e + 4), w("st", 255, 1024, 256), -1.0, AL.mult, 1024.0 + e, AL.add)
            copy("S" if e >= 2 else "V", w("gt", e, 256, 4), X, w("og", 4 * e, 4 * e + 4))
        quant("gq", "gs", 0, 128, w("gt"))
        send(t)
        if t == 0:
            for r in range(1, R):
                iota(w("fw", 2048 * (r - 1), 2048 * (r - 1) + 1024), [[1, 256], [0, 4]], 0, 0, [sent[0]])
                iota(w("cw", 768 * r, 768 * r + 256), [[0, 4], [1, K]], C + K * r, 0, [sent[0]])

        nbo = w("nbo", 16 * t, 16 * t + 16)
        if t:
            fwin, pwin = w("fw", 2048 * (t - 1), 2048 * t), w("pool", 0, 1024 + 256 * t)
            dma("Y", T.xc[:], ap(X), [X], [w("xc")], 1300.0)
            tt(w("fm"), w("b1", 0, 256), w("mzer"), AL.is_lt)
            scan(w("fs"), w("rs16"), w("fm"), -1.0, AL.max, AL.subtract)
            ts(w("of"), w("fs", 15, 256, 16), 1024.0, AL.mult, w("col", 8, 9), AL.add)
            tt(w("pm"), fwin, w("mmin"), AL.min, w("of"))
            scan(w("ps"), w("rmin"), w("pm"), -5e29, AL.min, AL.max)
            for e in range(4):
                oj = w("oj", 16 * e, 16 * e + 16)
                ts(oj, w("ps", 15, 256, 16), 4.0, AL.mult, float(e), AL.add)
                copy("S", w("g0", 256 * e, 256 * e + 256), pwin, oj)
                tt(w("jj", 2048 + e, 3072, 4), pwin, w("xc", e, 1024, 4), AL.max, oj)
            quant("jq", "js", 512, 768, w("jj", 2048, 3072))
            mm("b1", "u3q", "u3s", 128, "jq", "js", 512, 768)
            copy("S", w("cw", cw + 512, cw + 768), fwin, w("of"))
        else:
            for e in range(4):
                copy("S", w("g0", 256 * e, 256 * e + 256), w("pool", e, 1024, 4))
        copy("S", w("cw", cw + 256, cw + 512), w("cw", cw + 512, cw + 768), nbo)
        for e in range(4):
            tt(w("jj", 1024 + e, 2048, 4), w("g0", 256 * e, 256 * e + 256), w("pool", e, 1024, 4), AL.max, nbo)
        quant("jq", "js", 256, 512, w("jj", 1024, 2048))
        mm("b0", "u3q", "u3s", 128, "jq", "js", 256, 512)
        tt(w("s0m"), w("b1", 0, 256), w("mbig"), AL.max)
        tt(w("m01"), w("b0", 0, 256), w("s0m"), AL.max)
        tt(w("c1"), w("b0", 0, 256), w("s0m"), AL.is_gt)
        scan(w("c1s"), w("rs64"), w("c1"), -1.0, AL.max, AL.subtract)
        ts(w("bc"), w("c1s", 3, 256, 4), 0.5, AL.mult)

        arrive(t)
        for b in range(4):
            mm("b%d" % (4 + b), "eq", "es", 128 * b, "lq%d" % t, "ls%d" % t, 64, 192)
        for b in range(4):
            for u in range(4):
                tt(w("jj", 256 * u + b, 256 * u + 256, 4), w("b%d" % (4 + b), 64, 128), w("pool", 256 * u + b, 256 * u + 256, 4), AL.max)
            if t < R - 1:
                copy("S", w("pool", 1024 + 256 * t + b, 1280 + 256 * t, 4), w("b%d" % (4 + b), 64, 128))
        quant("jq", "js", 0, 256, w("jj", 0, 1024))
        mm("b2", "u3q", "u3s", 128, "jq", "js", 0, 256)
        tt(w("c2"), w("b2", 0, 256), w("m01"), AL.is_gt)
        scan(w("c2s"), w("rs128"), w("c2"), -1.0, AL.max, AL.subtract)
        tt(w("zz"), w("c2s", 3, 256, 4), w("bc"), AL.min)
        ts(w("oz"), w("zz"), 2048.0, AL.mult, w("col", 4, 5), AL.add)
        zv = PLAN["zv"]
        copy("S", w("zt", zv, 1024), w("jj"), w("oz", zv // 16, 64))
        copy("V", w("zt", 0, zv), w("jj"), w("oz", 0, zv // 16))
        quant("zq", "zs", 0, 256, w("zt"))
        ts(w("ow"), w("zz"), 512.0, AL.mult, w("col", 9, 10), AL.add)

        for b in range(4):
            mm("b%d" % (4 + b), "wq", "wsc", 128 * b, "zq", "zs", 0, 256)
        for b in range(4):
            act(w("rr", 256 * b, 256 * b + 256), w("b%d" % (4 + b), 0, 256), AF.Relu, 0.0, 0.015625)
            tt(w("pool", b, 1024, 4), w("rr", 256 * b, 256 * b + 256), w("pool", b, 1024, 4), AL.add)
        for h in range(4):
            o = ("fw", 2048 * t + 1024) if t < R - 1 else ("p4", 0)
            copy("S", w(o[0], o[1] + 256 * h, o[1] + 256 * h + 256), w("cw", cw, cw + 768), w("ow", 16 * h, 16 * h + 16))
        quant("xq", "xs", 0, 256, X)

    copy("S", w("po"), w("p4", 0, 1024, 4))
    mm("b0", "vq", "vs", 0, "xq", "xs", 0, 256)
    dma("Y", T.op[:], T.po[0:128:16, :], [w("po")], [])
    dma("Y", T.oc[:], T.xq[:].bitcast(dt.uint8), [w("xq")], [], 600.0)
    for k in range(4):
        dma("Y" if k < 2 else "S", T.osc[4 * k:4 * k + 4, :], T.xs[32 * k:32 * k + 4, :], [w("xs")], [])
    copy("V", w("yo"), w("b0", 0, 256))
    dma("S", T.y[:], T.yo[:], [w("yo")], [], 600.0)

    wake, m = PLAN["wake"], len(ops)
    pred, succ = [sorted(o["deps"] | o["soft"]) for o in ops], [[] for o in ops]
    for i in range(m):
        for d in pred[i]:
            succ[d].append(i)

    def deal(before, behind, prio, back):
        left, busy, begin, est = [len(b) for b in before], {}, [0.0] * m, [0.0] * m
        ready = [i for i in range(m) if not left[i]]
        while ready:
            i = max(ready, key=lambda j: (prio[j], -j))
            ready.remove(i)
            o = ops[i]
            at = est[i] + (o["lat"] if back else 0.0)
            slots = busy.setdefault(o["eng"], [])
            k = 0
            for k, (a, b) in enumerate(slots + [(1e18, 1e18)]):
                if at + o["cost"] <= a + 1e-6:
                    break
                at = max(at, b)
            slots.insert(k, (at, at + o["cost"]))
            begin[i] = at
            for s in behind[i]:
                est[s] = max(est[s], at + o["cost"] + (0.0 if back else o["lat"]) + wake)
                left[s] -= 1
                if not left[s]:
                    ready.append(s)
        return begin, max(begin[i] + ops[i]["cost"] + (0.0 if back else ops[i]["lat"]) for i in range(m))

    path = [0.0] * m
    for i in range(m - 1, -1, -1):
        path[i] = ops[i]["cost"] + ops[i]["lat"] + max([path[s] + wake for s in succ[i]] + [0.0])
    best = None
    for turn in range(PLAN["turns"]):
        begin, end = deal(pred, succ, path, False)
        if best is None or end < best[1]:
            best = (begin, end)
        rev = deal(succ, pred, [begin[i] + ops[i]["cost"] + ops[i]["lat"] for i in range(m)], True)[0]
        path = [rev[i] + ops[i]["cost"] for i in range(m)]
    seq = sorted(range(m), key=lambda i: (best[0][i], i))
    place = {i: k for k, i in enumerate(seq)}

    seen = {}
    for i in seq:
        o, latest = ops[i], {}
        for d in o["deps"]:
            key = ops[d]["eng"] if ops[d]["kind"] == "c" else ops[d]["sem"]
            if place[d] > place.get(latest.get(key), -1):
                latest[key] = d
        o["waits"] = []
        for key in sorted(latest):
            d = latest[key]
            if seen.get((o["eng"], key), -1) < place[d]:
                seen[(o["eng"], key)] = place[d]
                o["waits"].append(d)
                ops[d]["inc"] = True
    total = {}
    for i in seq:
        o = ops[i]
        if o["kind"] != "c":
            total[o["sem"]] = o["cnt"]
        elif o["inc"]:
            total[o["eng"]] = total.get(o["eng"], 0) + 1
            o["sem"], o["cnt"] = o["eng"], total[o["eng"]]
    for i in seq:
        o = ops[i]
        if o["kind"] == "a":
            continue
        for d in o["waits"]:
            queue[o["eng"]].wait_ge(T.sem[ops[d]["sem"]], ops[d]["cnt"])
        ins = o["fn"]()
        if o["kind"] == "d":
            ins.then_inc(T.sem[o["sem"]], 16)
        elif o["kind"] == "c" and o["inc"]:
            ins.then_inc(T.sem[o["sem"]], 1)
    for s in sorted(total):
        g.wait_ge(T.sem[s], total[s])
